import numpy as np
import ml_dtypes


def mxq(x, axis, fmt="e4m3"):
    dtype, down = {"e4m3": (ml_dtypes.float8_e4m3fn, 7), "e5m2": (ml_dtypes.float8_e5m2, 14)}[fmt]
    v = np.moveaxis(np.asarray(x, np.float32).astype(ml_dtypes.bfloat16).astype(np.float64), axis, -1)
    blocks = v.reshape(v.shape[:-1] + (-1, 32))
    amax = np.abs(blocks).max(-1, keepdims=True)
    byte = np.maximum(np.where(amax > 0, np.frexp(amax)[1] - 1 + 127, 0) - down, 1)
    scale = np.exp2(byte - 127.0)
    codes = (blocks / scale).astype(np.float32).astype(dtype).astype(np.float64)
    return np.moveaxis((codes * scale).reshape(v.shape), -1, axis)


WIDE = False


def mx_kscale(k):
    if not WIDE:
        return np.ones(k)
    levels = np.array([10, -10, 5, -5, 0])
    if k % 512:
        return np.exp2(np.random.permutation(np.resize(levels, k // 32))).repeat(32)
    a = np.empty((k // 512, 16))
    for p in range(k // 512):
        a[p, :8] = np.random.permutation(np.resize(levels, 8))
        for g in range(8):
            far = levels[np.abs(levels - a[p, g]) >= 10]
            a[p, g + 8] = far[np.random.randint(len(far))]
    return np.exp2(a.ravel()).repeat(32)


def f64(x):
    return np.asarray(x).astype(np.float64)


def striped8(idx):
    return np.asarray(idx).reshape(8, -1, 16).transpose(0, 2, 1).reshape(128, -1).astype(np.uint16)


def unstriped8(offs):
    return offs.reshape(8, 16, -1).transpose(0, 2, 1).reshape(8, -1).astype(np.int64)


def pick8(x, idx, run):
    r = np.arange(len(x))
    return x[r[:, None], idx[r % (8 * run) // run]]


E2M1 = np.array([0.0, 0.5, 1.0, 1.5, 2.0, 3.0, 4.0, 6.0, -0.0, -0.5, -1.0, -1.5, -2.0, -3.0, -4.0, -6.0])


def pack_weight(w, fmt):
    k, n = w.shape
    w = f64(np.asarray(w, np.float32).astype(ml_dtypes.bfloat16)).reshape(k // 32, 32, n)
    amax = np.abs(w).max(1)
    if fmt == "e4m3":
        byte = np.frexp(amax)[1] - 1 + 127 - 7
    else:
        mant, ex = np.frexp(amax / 6.0)
        byte = np.where(mant > 0.5, ex, ex - 1) + 127
    byte = np.clip(np.where(amax > 0, byte, 1), 1, 254)
    scaled = (w * np.exp2(127.0 - byte)[:, None, :]).reshape(k, n).astype(np.float32)
    by_word = np.ascontiguousarray(scaled.reshape(k // 512, 128, 4, n).transpose(0, 1, 3, 2))
    if fmt == "e4m3":
        words = by_word.astype(ml_dtypes.float8_e4m3fn).view(np.uint8)
    else:
        c = by_word.astype(ml_dtypes.float4_e2m1fn).view(np.uint8) & 0xF
        words = (c[..., 0::2] | (c[..., 1::2] << 4)).reshape(k // 512, 128, 2 * n)
    return np.ascontiguousarray(words), np.ascontiguousarray(byte.astype(np.uint8).reshape(k // 512, 16, n))


def unpack_weight(words, scales, fmt):
    g, _, n = scales.shape
    words = np.ascontiguousarray(words).reshape(g, 128, n, -1)
    if fmt == "e4m3":
        vals = words.view(ml_dtypes.float8_e4m3fn).astype(np.float64)
    else:
        nib = np.empty((g, 128, n, 4), np.uint8)
        nib[..., 0::2] = words & 0xF
        nib[..., 1::2] = words >> 4
        vals = E2M1[nib]
    vals = vals * np.repeat(np.exp2(scales.astype(np.float64) - 127.0), 8, axis=1)[..., None]
    return vals.transpose(0, 1, 3, 2).reshape(g * 512, n)


def softplus(v):
    return np.log(1.0 + np.exp(v))


D, T, I, Q = 512, 1024, 512, 128


def setup_inputs():
    n = np.random.standard_normal
    idx = np.stack([np.random.permutation(T)[:I] for _ in range(8)])
    idx2 = np.stack([np.random.permutation(T)[:I] for _ in range(8)])
    idx3 = np.stack([np.random.permutation(T)[:I] for _ in range(8)])
    fd = mx_kscale(D)
    keysp = pack_weight(n((D, T)) / fd[:, None], "e2m1")
    return {
        "query": (n((D, Q)) * 0.9 / np.sqrt(D) * fd[:, None]).astype(np.float32),
        "query2": (n((D, Q)) * 0.9 / np.sqrt(D) * fd[:, None]).astype(np.float32),
        "keys_words": keysp[0],
        "keys_scales": keysp[1],
        "lam": (np.random.uniform(1.0, 2.0, (Q, 1))).astype(np.float32),
        "old": (1.0 * n((Q, T))).astype(np.float32),
        "offs": striped8(idx),
        "offs2": striped8(idx2),
        "offs3": striped8(idx3),
    }


def reference(query, query2, keys_words, keys_scales, lam, old, offs, offs2, offs3):
    idx = unstriped8(offs)
    idx2 = unstriped8(offs2)
    idx3 = unstriped8(offs3)
    keysu = unpack_weight(keys_words, keys_scales, "e2m1")
    queryq = mxq(f64(query), 0, "e4m3")
    a = queryq.T @ keysu
    query2q = mxq(f64(query2), 0, "e4m3")
    b = query2q.T @ keysu
    ra = np.sqrt(softplus(pick8(a, idx, 16)) * softplus(pick8(b, idx, 16)) + 0.1)
    w = ra * f64(lam) - np.abs(pick8(a, idx, 16) - pick8(b, idx, 16))
    f1 = np.zeros((Q, T))
    f1[np.arange(Q)[:, None], idx[np.arange(Q) % 128 // 16]] = w
    f2 = f1 + f64(old)
    y = np.maximum(pick8(f2, idx2, 16), pick8(f2, idx3, 16))
    return y

@@ -1,0 +1,159 @@
+from contextlib import ExitStack
+
+import concourse.mybir as mybir
+
+F32 = mybir.dt.float32
+BF16 = mybir.dt.bfloat16
+I32 = mybir.dt.int32
+U32 = mybir.dt.uint32
+U16 = mybir.dt.uint16
+U8 = mybir.dt.uint8
+FP8X4 = mybir.dt.float8_e4m3fn_x4
+FP4X4 = mybir.dt.float4_e2m1fn_x4
+ALU = mybir.AluOpType
+ACT = mybir.ActivationFunctionType
+
+P = 128
+PACK = 4
+D, T, SLOTS, Q = 512, 1024, 512, 128
+N_PASS = 256
+HALF = SLOTS // 2
+EXP_CAP = 2.0**40
+
+FLOPS = 2 * 2 * D * Q * T
+
+
+def tile_attend_agreeingtwo_lean_throughtwo_heads_kernel(
+    tc, query, query2, keys_words, keys_scales, lam, old, offs, offs2, offs3, out
+):
+    nc = tc.nc
+    with ExitStack() as ctx:
+        sb = ctx.enter_context(tc.tile_pool(name="sb", bufs=1))
+        psum = ctx.enter_context(tc.psum_pool(name="psum", bufs=1))
+
+        def load_query(src, name):
+            raw = sb.tile([P, PACK, Q], F32, name=name + "_raw")
+            nc.sync.dma_start(out=raw[:], in_=src.rearrange("(p j) q -> p j q", j=PACK))
+            return raw
+
+        def quantise_query(raw, name, cast):
+            grouped = sb.tile([P, Q * PACK], BF16, name=name + "_bf", align_bytes=64)
+            cast(
+                grouped[:].rearrange("p (c i j) -> p c j i", i=4, j=PACK),
+                raw[:].rearrange("p j (c i) -> p c j i", i=4),
+            )
+            codes = sb.tile([P, Q], U32, name=name + "_codes", align_bytes=64)
+            scales = sb.tile([P, Q], U8, name=name + "_scales", align_bytes=64)
+            nc.vector.quantize_mx(out=codes[:].bitcast(FP8X4), scales=scales[:], in_=grouped[:])
+            return codes, scales
+
+        key_words = sb.tile([P, 2 * T], U8, align_bytes=64)
+        key_scales = sb.tile([P, T], U8, align_bytes=64)
+        list1 = sb.tile([P, SLOTS // 16], U16)
+        list2 = sb.tile([P, SLOTS // 16], U16)
+        list3 = sb.tile([P, SLOTS // 16], U16)
+        old_sb = sb.tile([P, T], F32)
+        lam_sb = sb.tile([P, 1], F32)
+        f1 = sb.tile([P, T], F32)
+
+        qa_raw = load_query(query, "qa")
+        for quad in range(4):
+            nc.scalar.dma_start(
+                out=key_scales[32 * quad : 32 * quad + 4, :].bitcast(I32),
+                in_=keys_scales[0, 4 * quad : 4 * quad + 4, :].bitcast(I32),
+            )
+        nc.sync.dma_start(out=key_words[:].bitcast(I32), in_=keys_words[0].bitcast(I32))
+        qb_raw = load_query(query2, "qb")
+        nc.sync.dma_start(list1[:], offs)
+        nc.sync.dma_start(out=lam_sb[:], in_=lam)
+        nc.sync.dma_start(out=old_sb[:], in_=old)
+        nc.sync.dma_start(list2[:], offs2)
+        nc.sync.dma_start(list3[:], offs3)
+        nc.vector.memset(f1[:], 0.0)
+
+        def scores(codes, scales, name, evacuate):
+            whole = sb.tile([P, T], F32, name=name)
+            for j in range(T // N_PASS):
+                cols = slice(j * N_PASS, (j + 1) * N_PASS)
+                bank = psum.tile([P, N_PASS], F32, name=f"{name}_bank{j}")
+                nc.tensor.matmul_mx(
+                    out=bank[:],
+                    lhsT=codes[:].bitcast(FP8X4),
+                    lhsT_scale=scales[:],
+                    rhs=key_words[:, 2 * cols.start : 2 * cols.stop].bitcast(FP4X4),
+                    rhs_scale=key_scales[:, cols],
+                    start=True,
+                    stop=True,
+                )
+                evacuate(whole[:, cols], bank[:])
+            return whole
+
+        def scalar_copy(dst, src):
+            nc.scalar.activation(dst, src, ACT.Copy)
+
+        qa = quantise_query(qa_raw, "qa", nc.vector.tensor_copy)
+        qb = quantise_query(qb_raw, "qb", scalar_copy)
+        a = scores(*qa, "a", scalar_copy)
+        b = scores(*qb, "b", nc.vector.tensor_copy)
+
+        def entries(lst, h):
+            return lst[:, h * HALF // 16 : (h + 1) * HALF // 16]
+
+        def part(h, which):
+            return slice((2 * h + which) * HALF, (2 * h + which + 1) * HALF)
+
+        def pair(h):
+            return slice(2 * h * HALF, 2 * (h + 1) * HALF)
+
+        def half(h):
+            return slice(h * HALF, (h + 1) * HALF)
+
+        first = sb.tile([P, 2 * SLOTS], F32)
+        picked_b = sb.tile([P, SLOTS], F32)
+        capped = sb.tile([P, 2 * SLOTS], F32)
+        logs = sb.tile([P, 2 * SLOTS], F32)
+        soft = sb.tile([P, 2 * SLOTS], F32)
+        diff = sb.tile([P, SLOTS], F32)
+        negabs = sb.tile([P, SLOTS], F32)
+        prod = sb.tile([P, SLOTS], F32)
+        ra = sb.tile([P, SLOTS], F32)
+        scaled = sb.tile([P, SLOTS], F32)
+
+        for h in range(2):
+            nc.scalar.activation(first[:, part(h, 0)], a[:].indirect(entries(list1, h)), ACT.Exp)
+        for h in range(2):
+            nc.vector.tensor_copy(picked_b[:, half(h)], b[:].indirect(entries(list1, h)))
+        nc.scalar.activation(first[:, part(1, 1)], b[:].indirect(entries(list1, 1)), ACT.Exp)
+        nc.scalar.activation(first[:, part(0, 1)], picked_b[:, half(0)], ACT.Exp)
+        nc.vector.tensor_scalar(capped[:], first[:], EXP_CAP, 1.0, ALU.min, ALU.add)
+        for h in range(2):
+            nc.scalar.activation(logs[:, pair(h)], capped[:, pair(h)], ACT.Ln)
+        for h in range(2):
+            nc.vector.tensor_copy(first[:, part(h, 0)], a[:].indirect(entries(list1, h)))
+        for h in range(2):
+            nc.vector.tensor_tensor(soft[:, part(h, 0)], first[:, part(h, 0)], logs[:, part(h, 0)], ALU.max)
+            nc.vector.tensor_tensor(soft[:, part(h, 1)], picked_b[:, half(h)], logs[:, part(h, 1)], ALU.max)
+        for h in range(2):
+            nc.vector.tensor_tensor(prod[:, half(h)], soft[:, part(h, 0)], soft[:, part(h, 1)], ALU.mult)
+        for h in range(2):
+            nc.vector.tensor_tensor(diff[:, half(h)], first[:, part(h, 0)], picked_b[:, half(h)], ALU.subtract)
+        nc.vector.scalar_tensor_tensor(negabs[:], diff[:], -1.0, diff[:], ALU.mult, ALU.min)
+        for h in range(2):
+            nc.scalar.activation(ra[:, half(h)], prod[:, half(h)], ACT.Sqrt, bias=0.1)
+            nc.scalar.activation(scaled[:, half(h)], ra[:, half(h)], ACT.Copy, scale=lam_sb[:, 0:1])
+            nc.vector.tensor_tensor(
+                f1[:].indirect(entries(list1, h)), scaled[:, half(h)], negabs[:, half(h)], ALU.add
+            )
+
+        f2 = sb.tile([P, T], F32)
+        nc.vector.tensor_tensor(f2[:], f1[:], old_sb[:], ALU.add)
+
+        at2 = sb.tile([P, SLOTS], F32)
+        at3 = sb.tile([P, SLOTS], F32)
+        best = sb.tile([P, SLOTS], F32)
+        for h in range(2):
+            nc.scalar.activation(at2[:, half(h)], f2[:].indirect(entries(list2, h)), ACT.Copy)
+            nc.vector.tensor_copy(at3[:, half(h)], f2[:].indirect(entries(list3, h)))
+        for h in range(2):
+            nc.vector.tensor_tensor(best[:, half(h)], at2[:, half(h)], at3[:, half(h)], ALU.max)
+            nc.sync.dma_start(out=out[:, half(h)], in_=best[:, half(h)])

@@ -36,12 +36,16 @@ def tile_attend_agreeingtwo_lean_throughtwo_heads_kernel(
             nc.sync.dma_start(out=raw[:], in_=src.rearrange("(p j) q -> p j q", j=PACK))
             return raw
 
-        def quantise_query(raw, name, cast):
+        def quantise_query(raw, name, casts):
             grouped = sb.tile([P, Q * PACK], BF16, name=name + "_bf", align_bytes=64)
-            cast(
-                grouped[:].rearrange("p (c i j) -> p c j i", i=4, j=PACK),
-                raw[:].rearrange("p j (c i) -> p c j i", i=4),
-            )
+            share = Q // len(casts)
+            for n, cast in enumerate(casts):
+                cast(
+                    grouped[:, n * share * PACK : (n + 1) * share * PACK].rearrange(
+                        "p (c i j) -> p c j i", i=4, j=PACK
+                    ),
+                    raw[:, :, n * share : (n + 1) * share].rearrange("p j (c i) -> p c j i", i=4),
+                )
             codes = sb.tile([P, Q], U32, name=name + "_codes", align_bytes=64)
             scales = sb.tile([P, Q], U8, name=name + "_scales", align_bytes=64)
             nc.vector.quantize_mx(out=codes[:].bitcast(FP8X4), scales=scales[:], in_=grouped[:])
@@ -58,12 +62,21 @@ def tile_attend_agreeingtwo_lean_throughtwo_heads_kernel(
 
         qa_raw = load_query(query, "qa")
         for quad in range(4):
-            nc.scalar.dma_start(
+            queue = nc.sync if quad < 2 else nc.scalar
+            queue.dma_start(
                 out=key_scales[32 * quad : 32 * quad + 4, :].bitcast(I32),
                 in_=keys_scales[0, 4 * quad : 4 * quad + 4, :].bitcast(I32),
             )
-        nc.sync.dma_start(out=key_words[:].bitcast(I32), in_=keys_words[0].bitcast(I32))
+
+        def load_key_words(n):
+            nc.sync.dma_start(
+                out=key_words[:, n * T : (n + 1) * T].bitcast(I32),
+                in_=keys_words[0, :, n * T : (n + 1) * T].bitcast(I32),
+            )
+
+        load_key_words(0)
         qb_raw = load_query(query2, "qb")
+        load_key_words(1)
         nc.sync.dma_start(list1[:], offs)
         nc.sync.dma_start(out=lam_sb[:], in_=lam)
         nc.sync.dma_start(out=old_sb[:], in_=old)
@@ -71,11 +84,13 @@ def tile_attend_agreeingtwo_lean_throughtwo_heads_kernel(
         nc.sync.dma_start(list3[:], offs3)
         nc.vector.memset(f1[:], 0.0)
 
-        def scores(codes, scales, name, evacuate):
+        def scores(codes, scales, name, first_bank, pieces):
             whole = sb.tile([P, T], F32, name=name)
-            for j in range(T // N_PASS):
-                cols = slice(j * N_PASS, (j + 1) * N_PASS)
-                bank = psum.tile([P, N_PASS], F32, name=f"{name}_bank{j}")
+            start = 0
+            for j, (width, evacuate) in enumerate(pieces):
+                cols = slice(start, start + width)
+                start = cols.stop
+                bank = psum.tile([P, width], F32, name=f"bank{(first_bank + j) % 8}")
                 nc.tensor.matmul_mx(
                     out=bank[:],
                     lhsT=codes[:].bitcast(FP8X4),
@@ -91,10 +106,12 @@ def tile_attend_agreeingtwo_lean_throughtwo_heads_kernel(
         def scalar_copy(dst, src):
             nc.scalar.activation(dst, src, ACT.Copy)
 
-        qa = quantise_query(qa_raw, "qa", nc.vector.tensor_copy)
-        qb = quantise_query(qb_raw, "qb", scalar_copy)
-        a = scores(*qa, "a", scalar_copy)
-        b = scores(*qb, "b", nc.vector.tensor_copy)
+        vector_copy = nc.vector.tensor_copy
+        qa = quantise_query(qa_raw, "qa", [vector_copy, scalar_copy])
+        qb = quantise_query(qb_raw, "qb", [scalar_copy])
+        a_pieces = [(256, scalar_copy), (256, scalar_copy), (256, vector_copy), (128, scalar_copy), (128, vector_copy)]
+        a = scores(*qa, "a", 0, a_pieces)
+        b = scores(*qb, "b", len(a_pieces), [(256, vector_copy)] * 4)
 
         def entries(lst, h):
             return lst[:, h * HALF // 16 : (h + 1) * HALF // 16]
@@ -116,7 +133,7 @@ def tile_attend_agreeingtwo_lean_throughtwo_heads_kernel(
         diff = sb.tile([P, SLOTS], F32)
         negabs = sb.tile([P, SLOTS], F32)
         prod = sb.tile([P, SLOTS], F32)
-        ra = sb.tile([P, SLOTS], F32)
+        ra = sb.tile([P, HALF], F32)
         scaled = sb.tile([P, SLOTS], F32)
 
         for h in range(2):
@@ -139,8 +156,11 @@ def tile_attend_agreeingtwo_lean_throughtwo_heads_kernel(
             nc.vector.tensor_tensor(diff[:, half(h)], first[:, part(h, 0)], picked_b[:, half(h)], ALU.subtract)
         nc.vector.scalar_tensor_tensor(negabs[:], diff[:], -1.0, diff[:], ALU.mult, ALU.min)
         for h in range(2):
-            nc.scalar.activation(ra[:, half(h)], prod[:, half(h)], ACT.Sqrt, bias=0.1)
-            nc.scalar.activation(scaled[:, half(h)], ra[:, half(h)], ACT.Copy, scale=lam_sb[:, 0:1])
+            runs = [slice(0, HALF // 2), slice(HALF // 2, HALF)]
+            for run in runs:
+                nc.scalar.activation(ra[:, run], prod[:, half(h)][:, run], ACT.Sqrt, bias=0.1)
+            for run in runs:
+                nc.scalar.activation(scaled[:, half(h)][:, run], ra[:, run], ACT.Copy, scale=lam_sb[:, 0:1])
             nc.vector.tensor_tensor(
                 f1[:].indirect(entries(list1, h)), scaled[:, half(h)], negabs[:, half(h)], ALU.add
             )

from contextlib import ExitStack

import concourse.mybir as mybir

F32 = mybir.dt.float32
BF16 = mybir.dt.bfloat16
I32 = mybir.dt.int32
U32 = mybir.dt.uint32
U16 = mybir.dt.uint16
U8 = mybir.dt.uint8
FP8X4 = mybir.dt.float8_e4m3fn_x4
FP4X4 = mybir.dt.float4_e2m1fn_x4
ALU = mybir.AluOpType
ACT = mybir.ActivationFunctionType

P = 128
PACK = 4
D, T, SLOTS, Q = 512, 1024, 512, 128
N_PASS = 256
HALF = SLOTS // 2
EXP_CAP = 2.0**40

FLOPS = 2 * 2 * D * Q * T


def tile_attend_agreeingtwo_lean_throughtwo_heads_kernel(
    tc, query, query2, keys_words, keys_scales, lam, old, offs, offs2, offs3, out
):
    nc = tc.nc
    with ExitStack() as ctx:
        sb = ctx.enter_context(tc.tile_pool(name="sb", bufs=1))
        psum = ctx.enter_context(tc.psum_pool(name="psum", bufs=1))

        def load_query(src, name):
            raw = sb.tile([P, PACK, Q], F32, name=name + "_raw")
            nc.sync.dma_start(out=raw[:], in_=src.rearrange("(p j) q -> p j q", j=PACK))
            return raw

        def quantise_query(raw, name, casts):
            grouped = sb.tile([P, Q * PACK], BF16, name=name + "_bf", align_bytes=64)
            share = Q // len(casts)
            for n, cast in enumerate(casts):
                cast(
                    grouped[:, n * share * PACK : (n + 1) * share * PACK].rearrange(
                        "p (c i j) -> p c j i", i=4, j=PACK
                    ),
                    raw[:, :, n * share : (n + 1) * share].rearrange("p j (c i) -> p c j i", i=4),
                )
            codes = sb.tile([P, Q], U32, name=name + "_codes", align_bytes=64)
            scales = sb.tile([P, Q], U8, name=name + "_scales", align_bytes=64)
            nc.vector.quantize_mx(out=codes[:].bitcast(FP8X4), scales=scales[:], in_=grouped[:])
            return codes, scales

        key_words = sb.tile([P, 2 * T], U8, align_bytes=64)
        key_scales = sb.tile([P, T], U8, align_bytes=64)
        list1 = sb.tile([P, SLOTS // 16], U16)
        list2 = sb.tile([P, SLOTS // 16], U16)
        list3 = sb.tile([P, SLOTS // 16], U16)
        old_sb = sb.tile([P, T], F32)
        lam_sb = sb.tile([P, 1], F32)
        f1 = sb.tile([P, T], F32)

        qa_raw = load_query(query, "qa")
        for quad in range(4):
            queue = nc.sync if quad < 2 else nc.scalar
            queue.dma_start(
                out=key_scales[32 * quad : 32 * quad + 4, :].bitcast(I32),
                in_=keys_scales[0, 4 * quad : 4 * quad + 4, :].bitcast(I32),
            )

        def load_key_words(n):
            nc.sync.dma_start(
                out=key_words[:, n * T : (n + 1) * T].bitcast(I32),
                in_=keys_words[0, :, n * T : (n + 1) * T].bitcast(I32),
            )

        load_key_words(0)
        qb_raw = load_query(query2, "qb")
        load_key_words(1)
        nc.sync.dma_start(list1[:], offs)
        nc.sync.dma_start(out=lam_sb[:], in_=lam)
        nc.sync.dma_start(out=old_sb[:], in_=old)
        nc.sync.dma_start(list2[:], offs2)
        nc.sync.dma_start(list3[:], offs3)
        nc.vector.memset(f1[:], 0.0)

        def scores(codes, scales, name, first_bank, pieces):
            whole = sb.tile([P, T], F32, name=name)
            start = 0
            for j, (width, evacuate) in enumerate(pieces):
                cols = slice(start, start + width)
                start = cols.stop
                bank = psum.tile([P, width], F32, name=f"bank{(first_bank + j) % 8}")
                nc.tensor.matmul_mx(
                    out=bank[:],
                    lhsT=codes[:].bitcast(FP8X4),
                    lhsT_scale=scales[:],
                    rhs=key_words[:, 2 * cols.start : 2 * cols.stop].bitcast(FP4X4),
                    rhs_scale=key_scales[:, cols],
                    start=True,
                    stop=True,
                )
                evacuate(whole[:, cols], bank[:])
            return whole

        def scalar_copy(dst, src):
            nc.scalar.activation(dst, src, ACT.Copy)

        vector_copy = nc.vector.tensor_copy
        qa = quantise_query(qa_raw, "qa", [vector_copy, scalar_copy])
        qb = quantise_query(qb_raw, "qb", [scalar_copy])
        a_pieces = [(256, scalar_copy), (256, scalar_copy), (256, vector_copy), (128, scalar_copy), (128, vector_copy)]
        a = scores(*qa, "a", 0, a_pieces)
        b = scores(*qb, "b", len(a_pieces), [(256, vector_copy)] * 4)

        def entries(lst, h):
            return lst[:, h * HALF // 16 : (h + 1) * HALF // 16]

        def part(h, which):
            return slice((2 * h + which) * HALF, (2 * h + which + 1) * HALF)

        def pair(h):
            return slice(2 * h * HALF, 2 * (h + 1) * HALF)

        def half(h):
            return slice(h * HALF, (h + 1) * HALF)

        first = sb.tile([P, 2 * SLOTS], F32)
        picked_b = sb.tile([P, SLOTS], F32)
        capped = sb.tile([P, 2 * SLOTS], F32)
        logs = sb.tile([P, 2 * SLOTS], F32)
        soft = sb.tile([P, 2 * SLOTS], F32)
        diff = sb.tile([P, SLOTS], F32)
        negabs = sb.tile([P, SLOTS], F32)
        prod = sb.tile([P, SLOTS], F32)
        ra = sb.tile([P, HALF], F32)
        scaled = sb.tile([P, SLOTS], F32)

        for h in range(2):
            nc.scalar.activation(first[:, part(h, 0)], a[:].indirect(entries(list1, h)), ACT.Exp)
        for h in range(2):
            nc.vector.tensor_copy(picked_b[:, half(h)], b[:].indirect(entries(list1, h)))
        nc.scalar.activation(first[:, part(1, 1)], b[:].indirect(entries(list1, 1)), ACT.Exp)
        nc.scalar.activation(first[:, part(0, 1)], picked_b[:, half(0)], ACT.Exp)
        nc.vector.tensor_scalar(capped[:], first[:], EXP_CAP, 1.0, ALU.min, ALU.add)
        for h in range(2):
            nc.scalar.activation(logs[:, pair(h)], capped[:, pair(h)], ACT.Ln)
        for h in range(2):
            nc.vector.tensor_copy(first[:, part(h, 0)], a[:].indirect(entries(list1, h)))
        for h in range(2):
            nc.vector.tensor_tensor(soft[:, part(h, 0)], first[:, part(h, 0)], logs[:, part(h, 0)], ALU.max)
            nc.vector.tensor_tensor(soft[:, part(h, 1)], picked_b[:, half(h)], logs[:, part(h, 1)], ALU.max)
        for h in range(2):
            nc.vector.tensor_tensor(prod[:, half(h)], soft[:, part(h, 0)], soft[:, part(h, 1)], ALU.mult)
        for h in range(2):
            nc.vector.tensor_tensor(diff[:, half(h)], first[:, part(h, 0)], picked_b[:, half(h)], ALU.subtract)
        nc.vector.scalar_tensor_tensor(negabs[:], diff[:], -1.0, diff[:], ALU.mult, ALU.min)
        for h in range(2):
            runs = [slice(0, HALF // 2), slice(HALF // 2, HALF)]
            for run in runs:
                nc.scalar.activation(ra[:, run], prod[:, half(h)][:, run], ACT.Sqrt, bias=0.1)
            for run in runs:
                nc.scalar.activation(scaled[:, half(h)][:, run], ra[:, run], ACT.Copy, scale=lam_sb[:, 0:1])
            nc.vector.tensor_tensor(
                f1[:].indirect(entries(list1, h)), scaled[:, half(h)], negabs[:, half(h)], ALU.add
            )

        f2 = sb.tile([P, T], F32)
        nc.vector.tensor_tensor(f2[:], f1[:], old_sb[:], ALU.add)

        at2 = sb.tile([P, SLOTS], F32)
        at3 = sb.tile([P, SLOTS], F32)
        best = sb.tile([P, SLOTS], F32)
        for h in range(2):
            nc.scalar.activation(at2[:, half(h)], f2[:].indirect(entries(list2, h)), ACT.Copy)
            nc.vector.tensor_copy(at3[:, half(h)], f2[:].indirect(entries(list3, h)))
        for h in range(2):
            nc.vector.tensor_tensor(best[:, half(h)], at2[:, half(h)], at3[:, half(h)], ALU.max)
            nc.sync.dma_start(out=out[:, half(h)], in_=best[:, half(h)])
